import numpy as np
import ml_dtypes


def mxq(x, axis, fmt="e4m3"):
    dtype, down = {"e4m3": (ml_dtypes.float8_e4m3fn, 7), "e5m2": (ml_dtypes.float8_e5m2, 14)}[fmt]
    v = np.moveaxis(np.asarray(x, np.float32).astype(ml_dtypes.bfloat16).astype(np.float64), axis, -1)
    blocks = v.reshape(v.shape[:-1] + (-1, 32))
    amax = np.abs(blocks).max(-1, keepdims=True)
    byte = np.maximum(np.where(amax > 0, np.frexp(amax)[1] - 1 + 127, 0) - down, 1)
    scale = np.exp2(byte - 127.0)
    codes = (blocks / scale).astype(np.float32).astype(dtype).astype(np.float64)
    return np.moveaxis((codes * scale).reshape(v.shape), -1, axis)


WIDE = False


def mx_kscale(k):
    if not WIDE:
        return np.ones(k)
    levels = np.array([10, -10, 5, -5, 0])
    if k % 512:
        return np.exp2(np.random.permutation(np.resize(levels, k // 32))).repeat(32)
    a = np.empty((k // 512, 16))
    for p in range(k // 512):
        a[p, :8] = np.random.permutation(np.resize(levels, 8))
        for g in range(8):
            far = levels[np.abs(levels - a[p, g]) >= 10]
            a[p, g + 8] = far[np.random.randint(len(far))]
    return np.exp2(a.ravel()).repeat(32)


BF16 = ml_dtypes.bfloat16


def bf(x):
    return np.asarray(x, np.float32).astype(BF16)


def f64(x):
    return np.asarray(x).astype(np.float64)


E2M1 = np.array([0.0, 0.5, 1.0, 1.5, 2.0, 3.0, 4.0, 6.0, -0.0, -0.5, -1.0, -1.5, -2.0, -3.0, -4.0, -6.0])


def pack_weight(w, fmt):
    k, n = w.shape
    w = f64(bf(w)).reshape(k // 32, 32, n)
    amax = np.abs(w).max(1)
    if fmt == "e4m3":
        byte = np.frexp(amax)[1] - 1 + 127 - 7
    else:
        mant, ex = np.frexp(amax / 6.0)
        byte = np.where(mant > 0.5, ex, ex - 1) + 127
    byte = np.clip(np.where(amax > 0, byte, 1), 1, 254)
    scaled = (w * np.exp2(127.0 - byte)[:, None, :]).reshape(k, n).astype(np.float32)
    by_word = np.ascontiguousarray(scaled.reshape(k // 512, 128, 4, n).transpose(0, 1, 3, 2))
    if fmt == "e4m3":
        words = by_word.astype(ml_dtypes.float8_e4m3fn).view(np.uint8)
    else:
        c = by_word.astype(ml_dtypes.float4_e2m1fn).view(np.uint8) & 0xF
        words = c[..., 0::2] | (c[..., 1::2] << 4)
    return np.ascontiguousarray(words), np.ascontiguousarray(byte.astype(np.uint8).reshape(k // 512, 16, n))


def unpack_weight(words, scales, fmt):
    g, p, n, _ = words.shape
    if fmt == "e4m3":
        vals = np.ascontiguousarray(words).view(ml_dtypes.float8_e4m3fn).astype(np.float64)
    else:
        nib = np.empty((g, p, n, 4), np.uint8)
        nib[..., 0::2] = words & 0xF
        nib[..., 1::2] = words >> 4
        vals = E2M1[nib]
    vals = vals * np.repeat(np.exp2(scales.astype(np.float64) - 127.0), 8, axis=1)[..., None]
    return vals.transpose(0, 1, 3, 2).reshape(g * 512, n)
def pack4(w):
    words, scales = pack_weight(w, "e2m1")
    return words.reshape(words.shape[0], 128, -1), scales


def unpack4(words, scales):
    return unpack_weight(words.reshape(words.shape[0], 128, -1, 2), scales, "e2m1")


M, K, N, D, R = 2048, 1024, 1024, 1024, 512


def setup_inputs():
    s, v, u = mx_kscale(K), mx_kscale(D), mx_kscale(M)
    c = np.random.uniform(0.5, 2.0, K)
    x = np.random.standard_normal((M, K)) * c * s * u[:, None]
    w = np.random.standard_normal((K, N)) / np.sqrt(K) / M ** 0.25 / s[:, None]
    ref = 0.5 * np.random.standard_normal((M, N)) / M ** 0.25 * u[:, None]
    a = np.random.standard_normal((D, M)) * v[:, None] / u
    b = np.random.standard_normal((D, R)) / np.sqrt(D) / M ** 0.25 / v[:, None]
    a_words, a_scales = pack4(a)
    b_words, b_scales = pack4(b)
    return {"x": bf(x), "inv_c": bf(1.0 / c), "w": bf(w), "ref": bf(ref),
            "a_words": a_words, "a_scales": a_scales,
            "b_words": b_words, "b_scales": b_scales}


def reference(x, inv_c, w, ref, a_words, a_scales, b_words, b_scales):
    xs = f64(x) * f64(inv_c)[None, :]
    y = mxq(xs, 1, "e4m3") @ mxq(f64(w), 0, "e4m3")
    e = y - f64(ref)
    a = unpack4(a_words, a_scales)
    b = unpack4(b_words, b_scales)
    f = np.maximum(a.T @ b, 0.0)
    return mxq(f, 0, "e4m3").T @ mxq(e, 0, "e4m3")

@@ -1,0 +1,340 @@
+from contextlib import ExitStack
+
+import concourse.mybir as mybir
+from concourse.masks import make_identity
+
+M, K, N, D, R = 2048, 1024, 1024, 1024, 512
+FLOPS = 2 * M * K * N + 2 * M * D * R + 2 * M * R * N
+
+F32 = mybir.dt.float32
+BF16 = mybir.dt.bfloat16
+I32 = mybir.dt.int32
+U32 = mybir.dt.uint32
+U8 = mybir.dt.uint8
+FP8X4 = mybir.dt.float8_e4m3fn_x4
+FP4X4 = mybir.dt.float4_e2m1fn_x4
+RELU = mybir.ActivationFunctionType.Relu
+MULT = mybir.AluOpType.mult
+SUB = mybir.AluOpType.subtract
+
+P = 128
+PACK = 4
+PASS = P * PACK
+GROUPS = M // PASS
+KP = K // PASS
+CH = 128
+HALF = 512
+RUN = 4
+
+
+def tile_smoothquant_error_moment_s12_kernel(
+    tc, x, inv_c, w, ref, a_words, a_scales, b_words, b_scales, out
+):
+    nc = tc.nc
+    with ExitStack() as ctx:
+        keep = ctx.enter_context(tc.tile_pool(name="keep", bufs=1))
+        stage = ctx.enter_context(tc.tile_pool(name="stage", bufs=3))
+        work = ctx.enter_context(tc.psum_pool(name="work", bufs=4))
+        moment = ctx.enter_context(tc.psum_pool(name="moment", bufs=1))
+        ctx.enter_context(tc.manual_schedule())
+
+        def kept(name, shape, dtype):
+            return keep.tile(shape, dtype, name=name, align_bytes=64)
+
+        b_codes = kept("b_codes", [P, KP, 2 * R], U8)
+        b_plane = kept("b_plane", [P, KP, R], U8)
+        a_rows = kept("a_rows", [P, KP, M // 4], I32)
+        a_raw = [kept("a_raw%d" % g, [P, KP, PASS // 2], I32) for g in range(GROUPS)]
+        a_codes = [kept("a_codes%d" % g, [P, KP, PACK, 2 * P], U8) for g in range(GROUPS)]
+        a_plane = [kept("a_plane%d" % g, [P, KP, PACK, P], U8) for g in range(GROUPS)]
+        x_raw = [kept("x_raw%d" % g, [P, PACK, K], BF16) for g in range(GROUPS)]
+        ref_raw = [kept("ref_raw%d" % g, [P, PACK, N], BF16) for g in range(GROUPS)]
+        w_raw = [kept("w_raw%d" % h, [P, KP, PACK, HALF], BF16) for h in range(N // HALF)]
+        inv = kept("inv", [P, KP, 2, 2], BF16)
+        ident = kept("ident", [P, P], F32)
+        xs_codes = [kept("xs_codes%d" % g, [P, KP, PASS], U32) for g in range(GROUPS)]
+        xs_plane = [kept("xs_plane%d" % g, [P, KP, PASS], U8) for g in range(GROUPS)]
+        w_codes = [kept("w_codes%d" % c, [P, KP, CH], U32) for c in range(N // CH)]
+        w_plane = [kept("w_plane%d" % c, [P, KP, CH], U8) for c in range(N // CH)]
+        f_codes = [kept("f_codes%d" % g, [P, R], U32) for g in range(GROUPS)]
+        f_plane = [kept("f_plane%d" % g, [P, R], U8) for g in range(GROUPS)]
+
+        nc.vector.memset(a_rows[:], 0)
+        nc.vector.memset(b_plane[:].rearrange("p g n -> p (g n)").bitcast(I32), 0)
+        make_identity(nc, ident[:])
+
+        a_words_g = a_words.bitcast(I32).rearrange("g p (G v) -> G p g v", G=GROUPS)
+        a_scale_rows = a_scales.bitcast(I32).rearrange("g (q r) v -> r q g v", r=4)
+        b_scale_rows = b_scales.bitcast(I32).rearrange("g (q r) v -> r q g v", r=4)
+        x_rows = x.rearrange("(G s t r) k -> G r s t k", G=GROUPS, t=PACK, r=RUN)
+        ref_rows = ref.rearrange("(G s t r) n -> G r s t n", G=GROUPS, t=PACK, r=RUN)
+        w_rows = w.rearrange("(g p j) n -> g p j n", g=KP, j=PACK)
+
+        def load_a(g):
+            nc.sync.dma_start(out=a_raw[g][:], in_=a_words_g[g])
+
+        def load_tokens(tiles, rows, g):
+            for r in range(RUN):
+                nc.sync.dma_start(out=tiles[g][r:P:RUN, :, :], in_=rows[g, r])
+
+        def load_w(h):
+            for g in range(KP):
+                nc.sync.dma_start(out=w_raw[h][:, g], in_=w_rows[g][:, :, h * HALF : (h + 1) * HALF])
+
+        nc.sync.dma_start(
+            out=b_codes[:].bitcast(I32), in_=b_words.bitcast(I32).rearrange("g p v -> p g v")
+        )
+        load_a(0)
+        for r in range(4):
+            nc.sync.dma_start(out=a_rows[r:P:32, :, :], in_=a_scale_rows[r])
+        for r in range(4):
+            nc.sync.dma_start(out=b_plane[r:P:32, :, :].bitcast(I32), in_=b_scale_rows[r])
+        load_tokens(x_raw, x_rows, 0)
+        nc.sync.dma_start(
+            out=inv[:].rearrange("p g u e -> p g (u e)"),
+            in_=inv_c.rearrange("(g p t) -> p g t", g=KP, t=PACK),
+        )
+        load_a(1)
+        load_w(0)
+        load_tokens(ref_raw, ref_rows, 0)
+        load_tokens(x_raw, x_rows, 1)
+        load_a(2)
+        load_tokens(ref_raw, ref_rows, 1)
+        load_tokens(x_raw, x_rows, 2)
+        load_a(3)
+        load_w(1)
+        load_tokens(ref_raw, ref_rows, 2)
+        load_tokens(x_raw, x_rows, 3)
+        load_tokens(ref_raw, ref_rows, 3)
+
+        def order_a(g):
+            nc.vector.tensor_copy(
+                out=a_codes[g][:].bitcast(I32).rearrange("p g t (s h) -> p g t s h", h=2),
+                in_=a_raw[g][:].rearrange("p g (s t h) -> p g t s h", t=PACK, h=2),
+            )
+            nc.vector.tensor_copy(
+                out=a_plane[g][:].bitcast(I32),
+                in_=a_rows[:, :, g * P : (g + 1) * P].rearrange("p g (s t) -> p g t s", t=PACK),
+            )
+
+        def quantize(codes, plane, values):
+            nc.vector.quantize_mx(out=codes.bitcast(FP8X4), scales=plane, in_=values)
+
+        f_values = {}
+
+        def features(g, c):
+            if c == 0:
+                f_values[g] = stage.tile([P, R, PACK], BF16, name="f_values", bufs=2, align_bytes=64)
+            bank = work.tile([P, PACK * CH], F32, name="bank")
+            for t in range(PACK):
+                for kp in range(KP):
+                    nc.tensor.matmul_mx(
+                        out=bank[:, t * CH : (t + 1) * CH],
+                        lhsT=a_codes[g][:, kp, t, :].bitcast(FP4X4),
+                        lhsT_scale=a_plane[g][:, kp, t, :],
+                        rhs=b_codes[:, kp, 2 * c * CH : 2 * (c + 1) * CH].bitcast(FP4X4),
+                        rhs_scale=b_plane[:, kp, c * CH : (c + 1) * CH],
+                        start=(kp == 0),
+                        stop=(kp == KP - 1),
+                    )
+            nc.scalar.activation(
+                out=f_values[g][:, c * CH : (c + 1) * CH, :],
+                in_=bank[:].rearrange("p (t n) -> p n t", t=PACK),
+                func=RELU,
+            )
+
+        def quantize_f(g):
+            quantize(f_codes[g][:], f_plane[g][:], f_values[g][:].rearrange("p n t -> p (n t)"))
+
+        x_sorted = {}
+
+        def sort_x(g, kp):
+            x_sorted[g, kp] = stage.tile([P, PACK, 2, P], F32, name="x_sorted")
+            words = x_raw[g][:].bitcast(F32)[:, :, kp * 2 * P : (kp + 1) * 2 * P]
+            nc.scalar.copy(out=x_sorted[g, kp][:], in_=words.rearrange("p t (v u) -> p t u v", u=2))
+
+        xs_values = {}
+
+        def turn_x(g, kp, pair):
+            if pair == 0:
+                xs_values[g, kp] = stage.tile([P, PASS, 2, 2], BF16, name="xs_values", align_bytes=64)
+            bank = work.tile([P, PACK * CH], F32, name="bank")
+            for u in range(2):
+                for tt in range(2):
+                    t = 2 * pair + tt
+                    if (g, kp) in x_sorted:
+                        words = x_sorted[g, kp][:, t, u, :]
+                    else:
+                        words = x_raw[g][:].bitcast(F32)[:, t, kp * 2 * P + u : (kp + 1) * 2 * P : 2]
+                    at = (2 * u + tt) * P
+                    nc.tensor.transpose(bank[:, at : at + P], words, ident[:])
+            nc.vector.tensor_tensor(
+                out=xs_values[g, kp][:, pair * 2 * P : (pair + 1) * 2 * P],
+                in0=bank[:].bitcast(BF16).rearrange("p (u m e) -> p m u e", u=2, e=2),
+                in1=inv[:, kp].unsqueeze(1).broadcast_to([P, 2 * P, 2, 2]),
+                op=MULT,
+            )
+
+        def quantize_xs(g, kp):
+            quantize(
+                xs_codes[g][:, kp, :],
+                xs_plane[g][:, kp, :],
+                xs_values[g, kp][:].rearrange("p m u e -> p (m u e)"),
+            )
+
+        w_values = {}
+
+        def interleave_w(c, on_vector):
+            w_values[c] = stage.tile([P, KP, CH, PACK], BF16, name="w_values", bufs=4, align_bytes=64)
+            h, n0 = divmod(c * CH, HALF)
+            dst = w_values[c][:].rearrange("p g (b i) j -> p g b j i", i=4)
+            src = w_raw[h][:, :, :, n0 : n0 + CH].rearrange("p g j (b i) -> p g b j i", i=4)
+            if on_vector:
+                nc.vector.tensor_copy(out=dst, in_=src)
+            else:
+                nc.scalar.copy(out=dst, in_=src)
+
+        def quantize_w(c):
+            quantize(
+                w_codes[c][:].rearrange("p g n -> p (g n)"),
+                w_plane[c][:].rearrange("p g n -> p (g n)"),
+                w_values[c][:].rearrange("p g n j -> p (g n j)"),
+            )
+
+        e_values, e_codes, e_plane = {}, {}, {}
+
+        def error(g, c):
+            h, n0 = divmod(c * CH, HALF)
+            if n0 == 0:
+                e_values[g, h] = stage.tile([P, HALF, PACK], BF16, name="e_values", bufs=2, align_bytes=64)
+            bank = work.tile([P, PACK * CH], F32, name="bank")
+            for t in range(PACK):
+                for kp in range(KP):
+                    nc.tensor.matmul_mx(
+                        out=bank[:, t * CH : (t + 1) * CH],
+                        lhsT=xs_codes[g][:, kp, t * P : (t + 1) * P].bitcast(FP8X4),
+                        lhsT_scale=xs_plane[g][:, kp, t * P : (t + 1) * P],
+                        rhs=w_codes[c][:, kp, :].bitcast(FP8X4),
+                        rhs_scale=w_plane[c][:, kp, :],
+                        start=(kp == 0),
+                        stop=(kp == KP - 1),
+                    )
+            nc.vector.tensor_tensor(
+                out=e_values[g, h][:, n0 : n0 + CH, :].rearrange("p (b i) t -> p b t i", i=4),
+                in0=bank[:].rearrange("p (t b i) -> p b t i", t=PACK, i=4),
+                in1=ref_raw[g][:, :, c * CH : (c + 1) * CH].rearrange("p t (b i) -> p b t i", i=4),
+                op=SUB,
+            )
+
+        def quantize_e(g, h):
+            e_codes[g, h] = stage.tile([P, HALF], U32, name="e_codes", bufs=5, align_bytes=64)
+            e_plane[g, h] = stage.tile([P, HALF], U8, name="e_plane", bufs=5, align_bytes=64)
+            quantize(e_codes[g, h][:], e_plane[g, h][:], e_values[g, h][:].rearrange("p n t -> p (n t)"))
+
+        sums = {}
+
+        def moment_pass(g, h, rt):
+            if g == 0:
+                sums[h, rt] = moment.tile([P, HALF], F32, name="sums%d" % rt)
+            nc.tensor.matmul_mx(
+                out=sums[h, rt][:],
+                lhsT=f_codes[g][:, rt * P : (rt + 1) * P].bitcast(FP8X4),
+                lhsT_scale=f_plane[g][:, rt * P : (rt + 1) * P],
+                rhs=e_codes[g, h][:].bitcast(FP8X4),
+                rhs_scale=e_plane[g, h][:],
+                start=(g == 0),
+                stop=(g == GROUPS - 1),
+            )
+
+        def moment_passes(g, h):
+            for rt in range(R // P):
+                moment_pass(g, h, rt)
+
+        def store(h, rt, on_vector):
+            result = stage.tile([P, HALF], F32, name="result", bufs=4)
+            if on_vector:
+                nc.vector.tensor_copy(out=result[:], in_=sums[h, rt][:])
+            else:
+                nc.scalar.copy(out=result[:], in_=sums[h, rt][:])
+            nc.sync.dma_start(out=out[rt * P : (rt + 1) * P, h * HALF : (h + 1) * HALF], in_=result[:])
+
+        def turn_group(g, first, second):
+            turn_x(g, 0, 0)
+            first()
+            turn_x(g, 0, 1)
+            turn_x(g, 1, 0)
+            quantize_xs(g, 0)
+            turn_x(g, 1, 1)
+            second()
+            quantize_xs(g, 1)
+
+        def error_half(g, h, between):
+            for c in range(4):
+                error(g, 4 * h + c)
+                if c < len(between):
+                    between[c]()
+
+        def nothing():
+            return None
+
+        order_a(0)
+        for c in range(4):
+            features(0, c)
+        order_a(1)
+        interleave_w(0, False)
+        interleave_w(1, False)
+        turn_group(0, nothing, lambda: quantize_f(0))
+        for c in range(4):
+            features(1, c)
+        interleave_w(2, True)
+        quantize_w(0)
+        interleave_w(3, True)
+        quantize_w(1)
+        quantize_w(2)
+        quantize_w(3)
+        sort_x(1, 0)
+        sort_x(1, 1)
+        error_half(0, 0, [lambda: order_a(2), lambda: quantize_f(1)])
+
+        turn_group(1, lambda: quantize_e(0, 0), nothing)
+        for c in range(4):
+            features(2, c)
+        sort_x(2, 0)
+        sort_x(2, 1)
+        interleave_w(4, False)
+        interleave_w(5, False)
+        error_half(1, 0, [lambda: order_a(3), lambda: quantize_f(2)])
+        moment_passes(0, 0)
+
+        turn_group(2, lambda: quantize_e(1, 0), lambda: quantize_w(4))
+        for c in range(4):
+            features(3, c)
+        sort_x(3, 0)
+        sort_x(3, 1)
+        interleave_w(6, False)
+        interleave_w(7, False)
+        error_half(2, 0, [lambda: quantize_w(5), lambda: quantize_f(3)])
+        moment_passes(1, 0)
+
+        turn_group(3, lambda: quantize_e(2, 0), lambda: quantize_w(6))
+        quantize_w(7)
+        error_half(0, 1, [])
+        moment_passes(2, 0)
+        error_half(3, 0, [lambda: quantize_e(0, 1)])
+        error_half(1, 1, [lambda: quantize_e(3, 0)])
+        moment_passes(3, 0)
+        for rt in range(R // P):
+            store(0, rt, False)
+        error_half(2, 1, [lambda: quantize_e(1, 1)])
+        moment_passes(0, 1)
+        error_half(3, 1, [lambda: quantize_e(2, 1)])
+        quantize_e(3, 1)
+        for rt in range(3):
+            moment_pass(1, 1, rt)
+            moment_pass(2, 1, rt)
+        for rt in range(3):
+            moment_pass(3, 1, rt)
+            store(1, rt, rt == 1)
+        for g in range(1, GROUPS):
+            moment_pass(g, 1, 3)
+        store(1, 3, True)

@@ -14,6 +14,7 @@ U8 = mybir.dt.uint8
 FP8X4 = mybir.dt.float8_e4m3fn_x4
 FP4X4 = mybir.dt.float4_e2m1fn_x4
 RELU = mybir.ActivationFunctionType.Relu
+COPY = mybir.ActivationFunctionType.Copy
 MULT = mybir.AluOpType.mult
 SUB = mybir.AluOpType.subtract
 
@@ -25,6 +26,7 @@ KP = K // PASS
 CH = 128
 HALF = 512
 RUN = 4
+WALK = 4
 
 
 def tile_smoothquant_error_moment_s12_kernel(
@@ -43,7 +45,8 @@ def tile_smoothquant_error_moment_s12_kernel(
 
         b_codes = kept("b_codes", [P, KP, 2 * R], U8)
         b_plane = kept("b_plane", [P, KP, R], U8)
-        a_rows = kept("a_rows", [P, KP, M // 4], I32)
+        a_rows_first = kept("a_rows_first", [P, KP, 2 * P], I32)
+        a_rows_rest = kept("a_rows_rest", [P, KP, 2 * P], I32)
         a_raw = [kept("a_raw%d" % g, [P, KP, PASS // 2], I32) for g in range(GROUPS)]
         a_codes = [kept("a_codes%d" % g, [P, KP, PACK, 2 * P], U8) for g in range(GROUPS)]
         a_plane = [kept("a_plane%d" % g, [P, KP, PACK, P], U8) for g in range(GROUPS)]
@@ -59,8 +62,9 @@ def tile_smoothquant_error_moment_s12_kernel(
         f_codes = [kept("f_codes%d" % g, [P, R], U32) for g in range(GROUPS)]
         f_plane = [kept("f_plane%d" % g, [P, R], U8) for g in range(GROUPS)]
 
-        nc.vector.memset(a_rows[:], 0)
-        nc.vector.memset(b_plane[:].rearrange("p g n -> p (g n)").bitcast(I32), 0)
+        nc.vector.memset(a_rows_first[:], 0)
+        nc.vector.memset(a_rows_rest[:], 0)
+        nc.gpsimd.memset(b_plane[:].rearrange("p g n -> p (g n)").bitcast(I32), 0)
         make_identity(nc, ident[:])
 
         a_words_g = a_words.bitcast(I32).rearrange("g p (G v) -> G p g v", G=GROUPS)
@@ -81,40 +85,56 @@ def tile_smoothquant_error_moment_s12_kernel(
             for g in range(KP):
                 nc.sync.dma_start(out=w_raw[h][:, g], in_=w_rows[g][:, :, h * HALF : (h + 1) * HALF])
 
-        nc.sync.dma_start(
-            out=b_codes[:].bitcast(I32), in_=b_words.bitcast(I32).rearrange("g p v -> p g v")
-        )
-        load_a(0)
-        for r in range(4):
-            nc.sync.dma_start(out=a_rows[r:P:32, :, :], in_=a_scale_rows[r])
-        for r in range(4):
-            nc.sync.dma_start(out=b_plane[r:P:32, :, :].bitcast(I32), in_=b_scale_rows[r])
+        def load_b():
+            nc.sync.dma_start(
+                out=b_codes[:].bitcast(I32), in_=b_words.bitcast(I32).rearrange("g p v -> p g v")
+            )
+
+        def load_a_scales(rows, first, count):
+            for r in range(4):
+                nc.sync.dma_start(
+                    out=rows[r:P:32, :, :], in_=a_scale_rows[r][:, :, first * P : (first + count) * P]
+                )
+
+        def load_b_scales():
+            for r in range(4):
+                nc.gpsimd.dma_start(out=b_plane[r:P:32, :, :].bitcast(I32), in_=b_scale_rows[r])
+
+        def load_inv():
+            nc.sync.dma_start(
+                out=inv[:].rearrange("p g u e -> p g (u e)"),
+                in_=inv_c.rearrange("(g p t) -> p g t", g=KP, t=PACK),
+            )
+
+        load_b_scales()
         load_tokens(x_raw, x_rows, 0)
-        nc.sync.dma_start(
-            out=inv[:].rearrange("p g u e -> p g (u e)"),
-            in_=inv_c.rearrange("(g p t) -> p g t", g=KP, t=PACK),
-        )
-        load_a(1)
+        load_inv()
+        load_a(0)
+        load_b()
+        load_a_scales(a_rows_first, 0, 2)
         load_w(0)
+        load_a(1)
         load_tokens(ref_raw, ref_rows, 0)
         load_tokens(x_raw, x_rows, 1)
-        load_a(2)
         load_tokens(ref_raw, ref_rows, 1)
         load_tokens(x_raw, x_rows, 2)
-        load_a(3)
+        load_a(2)
+        load_a_scales(a_rows_rest, 2, 2)
         load_w(1)
         load_tokens(ref_raw, ref_rows, 2)
         load_tokens(x_raw, x_rows, 3)
+        load_a(3)
         load_tokens(ref_raw, ref_rows, 3)
 
         def order_a(g):
+            rows = (a_rows_first, a_rows_rest)[g // 2][:, :, g % 2 * P : (g % 2 + 1) * P]
             nc.vector.tensor_copy(
                 out=a_codes[g][:].bitcast(I32).rearrange("p g t (s h) -> p g t s h", h=2),
                 in_=a_raw[g][:].rearrange("p g (s t h) -> p g t s h", t=PACK, h=2),
             )
             nc.vector.tensor_copy(
                 out=a_plane[g][:].bitcast(I32),
-                in_=a_rows[:, :, g * P : (g + 1) * P].rearrange("p g (s t) -> p g t s", t=PACK),
+                in_=rows.rearrange("p g (s t) -> p g t s", t=PACK),
             )
 
         def quantize(codes, plane, values):
@@ -189,7 +209,10 @@ def tile_smoothquant_error_moment_s12_kernel(
             h, n0 = divmod(c * CH, HALF)
             dst = w_values[c][:].rearrange("p g (b i) j -> p g b j i", i=4)
             src = w_raw[h][:, :, :, n0 : n0 + CH].rearrange("p g j (b i) -> p g b j i", i=4)
-            if on_vector:
+            if c == 0:
+                for kp in range(KP):
+                    nc.scalar.activation(out=dst[:, kp], in_=src[:, kp], func=COPY)
+            elif on_vector:
                 nc.vector.tensor_copy(out=dst, in_=src)
             else:
                 nc.scalar.copy(out=dst, in_=src)
@@ -203,10 +226,11 @@ def tile_smoothquant_error_moment_s12_kernel(
 
         e_values, e_codes, e_plane = {}, {}, {}
 
-        def error(g, c):
-            h, n0 = divmod(c * CH, HALF)
-            if n0 == 0:
-                e_values[g, h] = stage.tile([P, HALF, PACK], BF16, name="e_values", bufs=2, align_bytes=64)
+        def error(g, c, span):
+            n0, width = span
+            at = c * CH - n0
+            if at == 0:
+                e_values[g, n0] = stage.tile([P, width, PACK], BF16, name="e_values", bufs=3, align_bytes=64)
             bank = work.tile([P, PACK * CH], F32, name="bank")
             for t in range(PACK):
                 for kp in range(KP):
@@ -220,121 +244,126 @@ def tile_smoothquant_error_moment_s12_kernel(
                         stop=(kp == KP - 1),
                     )
             nc.vector.tensor_tensor(
-                out=e_values[g, h][:, n0 : n0 + CH, :].rearrange("p (b i) t -> p b t i", i=4),
-                in0=bank[:].rearrange("p (t b i) -> p b t i", t=PACK, i=4),
-                in1=ref_raw[g][:, :, c * CH : (c + 1) * CH].rearrange("p t (b i) -> p b t i", i=4),
+                out=e_values[g, n0][:, at : at + CH, :].rearrange("p (b i) t -> p b t i", i=WALK),
+                in0=bank[:].rearrange("p (t b i) -> p b t i", t=PACK, i=WALK),
+                in1=ref_raw[g][:, :, c * CH : (c + 1) * CH].rearrange("p t (b i) -> p b t i", i=WALK),
                 op=SUB,
             )
 
-        def quantize_e(g, h):
-            e_codes[g, h] = stage.tile([P, HALF], U32, name="e_codes", bufs=5, align_bytes=64)
-            e_plane[g, h] = stage.tile([P, HALF], U8, name="e_plane", bufs=5, align_bytes=64)
-            quantize(e_codes[g, h][:], e_plane[g, h][:], e_values[g, h][:].rearrange("p n t -> p (n t)"))
+        def quantize_e(g, span):
+            n0, width = span
+            e_codes[g, n0] = stage.tile([P, width], U32, name="e_codes", bufs=5, align_bytes=64)
+            e_plane[g, n0] = stage.tile([P, width], U8, name="e_plane", bufs=5, align_bytes=64)
+            quantize(e_codes[g, n0][:], e_plane[g, n0][:], e_values[g, n0][:].rearrange("p n t -> p (n t)"))
 
         sums = {}
 
-        def moment_pass(g, h, rt):
+        def moment_pass(g, span, rt):
+            n0, width = span
             if g == 0:
-                sums[h, rt] = moment.tile([P, HALF], F32, name="sums%d" % rt)
+                sums[n0, rt] = moment.tile([P, HALF], F32, name="sums%d" % rt)
             nc.tensor.matmul_mx(
-                out=sums[h, rt][:],
+                out=sums[n0, rt][:, 0:width],
                 lhsT=f_codes[g][:, rt * P : (rt + 1) * P].bitcast(FP8X4),
                 lhsT_scale=f_plane[g][:, rt * P : (rt + 1) * P],
-                rhs=e_codes[g, h][:].bitcast(FP8X4),
-                rhs_scale=e_plane[g, h][:],
+                rhs=e_codes[g, n0][:].bitcast(FP8X4),
+                rhs_scale=e_plane[g, n0][:],
                 start=(g == 0),
                 stop=(g == GROUPS - 1),
             )
 
-        def moment_passes(g, h):
+        def moment_passes(g, span):
             for rt in range(R // P):
-                moment_pass(g, h, rt)
+                moment_pass(g, span, rt)
 
-        def store(h, rt, on_vector):
-            result = stage.tile([P, HALF], F32, name="result", bufs=4)
+        def store(span, rt, on_vector):
+            n0, width = span
+            result = stage.tile([P, width], F32, name="result", bufs=4)
             if on_vector:
-                nc.vector.tensor_copy(out=result[:], in_=sums[h, rt][:])
+                nc.vector.tensor_copy(out=result[:], in_=sums[n0, rt][:, 0:width])
             else:
-                nc.scalar.copy(out=result[:], in_=sums[h, rt][:])
-            nc.sync.dma_start(out=out[rt * P : (rt + 1) * P, h * HALF : (h + 1) * HALF], in_=result[:])
+                nc.scalar.copy(out=result[:], in_=sums[n0, rt][:, 0:width])
+            nc.sync.dma_start(out=out[rt * P : (rt + 1) * P, n0 : n0 + width], in_=result[:])
 
-        def turn_group(g, first, second):
-            turn_x(g, 0, 0)
-            first()
-            turn_x(g, 0, 1)
-            turn_x(g, 1, 0)
-            quantize_xs(g, 0)
-            turn_x(g, 1, 1)
-            second()
-            quantize_xs(g, 1)
+        def errors(g, span, between):
+            n0, width = span
+            for i in range(width // CH):
+                error(g, n0 // CH + i, span)
+                for step in between.get(i, ()):
+                    step()
 
-        def error_half(g, h, between):
-            for c in range(4):
-                error(g, 4 * h + c)
-                if c < len(between):
-                    between[c]()
+        def turn_group(g, between):
+            for i in range(4):
+                turn_x(g, i // 2, i % 2)
+                for step in between.get(i, ()):
+                    step()
 
-        def nothing():
-            return None
+        def do(fn, *args):
+            return lambda: fn(*args)
 
-        order_a(0)
-        for c in range(4):
-            features(0, c)
-        order_a(1)
+        first, third, last = (0, 512), (512, 256), (768, 256)
+        sort_x(0, 1)
+        turn_group(0, {0: [do(order_a, 0)]})
         interleave_w(0, False)
         interleave_w(1, False)
-        turn_group(0, nothing, lambda: quantize_f(0))
         for c in range(4):
-            features(1, c)
+            features(0, c)
+        quantize_xs(0, 0)
         interleave_w(2, True)
+        quantize_xs(0, 1)
         quantize_w(0)
         interleave_w(3, True)
         quantize_w(1)
         quantize_w(2)
         quantize_w(3)
-        sort_x(1, 0)
+        order_a(1)
         sort_x(1, 1)
-        error_half(0, 0, [lambda: order_a(2), lambda: quantize_f(1)])
 
-        turn_group(1, lambda: quantize_e(0, 0), nothing)
-        for c in range(4):
-            features(2, c)
-        sort_x(2, 0)
-        sort_x(2, 1)
-        interleave_w(4, False)
-        interleave_w(5, False)
-        error_half(1, 0, [lambda: order_a(3), lambda: quantize_f(2)])
-        moment_passes(0, 0)
+        for g in range(GROUPS - 1):
+            errors(g, first, {})
+            turn_group(g + 1, {})
+            if g > 0:
+                moment_passes(g - 1, first)
+                interleave_w(2 + 2 * g, False)
+                interleave_w(3 + 2 * g, False)
+            for c in range(4):
+                features(g + 1, c)
+            quantize_xs(g + 1, 0)
+            quantize_xs(g + 1, 1)
+            quantize_e(g, first)
+            quantize_f(g)
+            if g + 2 < GROUPS:
+                sort_x(g + 2, 0)
+                sort_x(g + 2, 1)
+                order_a(g + 2)
+            else:
+                quantize_w(4)
+                quantize_w(5)
 
-        turn_group(2, lambda: quantize_e(1, 0), lambda: quantize_w(4))
-        for c in range(4):
-            features(3, c)
-        sort_x(3, 0)
-        sort_x(3, 1)
-        interleave_w(6, False)
-        interleave_w(7, False)
-        error_half(2, 0, [lambda: quantize_w(5), lambda: quantize_f(3)])
-        moment_passes(1, 0)
-
-        turn_group(3, lambda: quantize_e(2, 0), lambda: quantize_w(6))
-        quantize_w(7)
-        error_half(0, 1, [])
-        moment_passes(2, 0)
-        error_half(3, 0, [lambda: quantize_e(0, 1)])
-        error_half(1, 1, [lambda: quantize_e(3, 0)])
-        moment_passes(3, 0)
-        for rt in range(R // P):
-            store(0, rt, False)
-        error_half(2, 1, [lambda: quantize_e(1, 1)])
-        moment_passes(0, 1)
-        error_half(3, 1, [lambda: quantize_e(2, 1)])
-        quantize_e(3, 1)
-        for rt in range(3):
-            moment_pass(1, 1, rt)
-            moment_pass(2, 1, rt)
-        for rt in range(3):
-            moment_pass(3, 1, rt)
-            store(1, rt, rt == 1)
-        for g in range(1, GROUPS):
-            moment_pass(g, 1, 3)
-        store(1, 3, True)
+        errors(3, first, {})
+        moment_passes(2, first)
+        quantize_f(3)
+        quantize_e(3, first)
+        errors(0, third, {})
+        errors(1, third, {0: [do(quantize_e, 0, third)]})
+        moment_passes(3, first)
+        for rt in range(4):
+            store(first, rt, False)
+        errors(2, third, {0: [do(quantize_e, 1, third), do(quantize_w, 6)]})
+        errors(3, third, {0: [do(quantize_e, 2, third), do(quantize_w, 7)]})
+        moment_passes(0, third)
+        moment_passes(1, third)
+        errors(0, last, {0: [do(quantize_e, 3, third)]})
+        moment_passes(2, third)
+        errors(1, last, {0: [do(quantize_e, 0, last)]})
+        moment_passes(3, third)
+        for rt in range(4):
+            store(third, rt, False)
+        errors(2, last, {0: [do(quantize_e, 1, last)]})
+        errors(3, last, {0: [do(quantize_e, 2, last)]})
+        quantize_e(3, last)
+        for g in range(3):
+            moment_passes(g, last)
+        for rt in range(4):
+            moment_pass(3, last, rt)
+            store(last, rt, rt % 2 == 1)

@@ -26,7 +26,7 @@ KP = K // PASS
 CH = 128
 HALF = 512
 RUN = 4
-WALK = 4
+WALK = 2
 
 
 def tile_smoothquant_error_moment_s12_kernel(
@@ -51,7 +51,11 @@ def tile_smoothquant_error_moment_s12_kernel(
         a_codes = [kept("a_codes%d" % g, [P, KP, PACK, 2 * P], U8) for g in range(GROUPS)]
         a_plane = [kept("a_plane%d" % g, [P, KP, PACK, P], U8) for g in range(GROUPS)]
         x_raw = [kept("x_raw%d" % g, [P, PACK, K], BF16) for g in range(GROUPS)]
-        ref_raw = [kept("ref_raw%d" % g, [P, PACK, N], BF16) for g in range(GROUPS)]
+        ref_raw = {
+            (g, h): kept("ref_raw%d_%d" % (g, h), [P, PACK, HALF], BF16)
+            for g in range(GROUPS)
+            for h in range(N // HALF)
+        }
         w_raw = [kept("w_raw%d" % h, [P, KP, PACK, HALF], BF16) for h in range(N // HALF)]
         inv = kept("inv", [P, KP, 2, 2], BF16)
         ident = kept("ident", [P, P], F32)
@@ -81,9 +85,14 @@ def tile_smoothquant_error_moment_s12_kernel(
             for r in range(RUN):
                 nc.sync.dma_start(out=tiles[g][r:P:RUN, :, :], in_=rows[g, r])
 
-        def load_w(h):
-            for g in range(KP):
-                nc.sync.dma_start(out=w_raw[h][:, g], in_=w_rows[g][:, :, h * HALF : (h + 1) * HALF])
+        def load_ref(g, h):
+            for r in range(RUN):
+                nc.sync.dma_start(
+                    out=ref_raw[g, h][r:P:RUN, :, :], in_=ref_rows[g, r][:, :, h * HALF : (h + 1) * HALF]
+                )
+
+        def load_w(h, g):
+            nc.sync.dma_start(out=w_raw[h][:, g], in_=w_rows[g][:, :, h * HALF : (h + 1) * HALF])
 
         def load_b():
             nc.sync.dma_start(
@@ -98,7 +107,7 @@ def tile_smoothquant_error_moment_s12_kernel(
 
         def load_b_scales():
             for r in range(4):
-                nc.gpsimd.dma_start(out=b_plane[r:P:32, :, :].bitcast(I32), in_=b_scale_rows[r])
+                nc.sync.dma_start(out=b_plane[r:P:32, :, :].bitcast(I32), in_=b_scale_rows[r])
 
         def load_inv():
             nc.sync.dma_start(
@@ -106,25 +115,29 @@ def tile_smoothquant_error_moment_s12_kernel(
                 in_=inv_c.rearrange("(g p t) -> p g t", g=KP, t=PACK),
             )
 
-        load_b_scales()
         load_tokens(x_raw, x_rows, 0)
+        load_a_scales(a_rows_first, 0, 2)
         load_inv()
         load_a(0)
         load_b()
-        load_a_scales(a_rows_first, 0, 2)
-        load_w(0)
+        load_w(0, 0)
+        load_b_scales()
+        load_w(0, 1)
         load_a(1)
-        load_tokens(ref_raw, ref_rows, 0)
+        load_ref(0, 0)
         load_tokens(x_raw, x_rows, 1)
-        load_tokens(ref_raw, ref_rows, 1)
         load_tokens(x_raw, x_rows, 2)
         load_a(2)
         load_a_scales(a_rows_rest, 2, 2)
-        load_w(1)
-        load_tokens(ref_raw, ref_rows, 2)
+        load_ref(1, 0)
         load_tokens(x_raw, x_rows, 3)
         load_a(3)
-        load_tokens(ref_raw, ref_rows, 3)
+        load_ref(2, 0)
+        load_w(1, 0)
+        load_w(1, 1)
+        load_ref(3, 0)
+        for g in range(GROUPS):
+            load_ref(g, 1)
 
         def order_a(g):
             rows = (a_rows_first, a_rows_rest)[g // 2][:, :, g % 2 * P : (g % 2 + 1) * P]
@@ -133,8 +146,8 @@ def tile_smoothquant_error_moment_s12_kernel(
                 in_=a_raw[g][:].rearrange("p g (s t h) -> p g t s h", t=PACK, h=2),
             )
             nc.vector.tensor_copy(
-                out=a_plane[g][:].bitcast(I32),
-                in_=rows.rearrange("p g (s t) -> p g t s", t=PACK),
+                out=a_plane[g][:].bitcast(I32).rearrange("p g t (b i) -> p g b t i", i=4),
+                in_=rows.rearrange("p g (b i t) -> p g b t i", i=4, t=PACK),
             )
 
         def quantize(codes, plane, values):
@@ -246,7 +259,7 @@ def tile_smoothquant_error_moment_s12_kernel(
             nc.vector.tensor_tensor(
                 out=e_values[g, n0][:, at : at + CH, :].rearrange("p (b i) t -> p b t i", i=WALK),
                 in0=bank[:].rearrange("p (t b i) -> p b t i", t=PACK, i=WALK),
-                in1=ref_raw[g][:, :, c * CH : (c + 1) * CH].rearrange("p t (b i) -> p b t i", i=WALK),
+                in1=ref_raw[g, c * CH // HALF][:, :, c * CH % HALF : c * CH % HALF + CH].rearrange("p t (b i) -> p b t i", i=WALK),
                 op=SUB,
             )
 
@@ -324,8 +337,9 @@ def tile_smoothquant_error_moment_s12_kernel(
             turn_group(g + 1, {})
             if g > 0:
                 moment_passes(g - 1, first)
-                interleave_w(2 + 2 * g, False)
-                interleave_w(3 + 2 * g, False)
+            if g + 2 == GROUPS:
+                interleave_w(4, False)
+                interleave_w(5, False)
             for c in range(4):
                 features(g + 1, c)
             quantize_xs(g + 1, 0)
@@ -340,6 +354,8 @@ def tile_smoothquant_error_moment_s12_kernel(
                 quantize_w(4)
                 quantize_w(5)
 
+        interleave_w(6, False)
+        interleave_w(7, False)
         errors(3, first, {})
         moment_passes(2, first)
         quantize_f(3)

from contextlib import ExitStack

import concourse.mybir as mybir
from concourse.masks import make_identity

M, K, N, D, R = 2048, 1024, 1024, 1024, 512
FLOPS = 2 * M * K * N + 2 * M * D * R + 2 * M * R * N

F32 = mybir.dt.float32
BF16 = mybir.dt.bfloat16
I32 = mybir.dt.int32
U32 = mybir.dt.uint32
U8 = mybir.dt.uint8
FP8X4 = mybir.dt.float8_e4m3fn_x4
FP4X4 = mybir.dt.float4_e2m1fn_x4
RELU = mybir.ActivationFunctionType.Relu
COPY = mybir.ActivationFunctionType.Copy
MULT = mybir.AluOpType.mult
SUB = mybir.AluOpType.subtract

P = 128
PACK = 4
PASS = P * PACK
GROUPS = M // PASS
KP = K // PASS
CH = 128
HALF = 512
RUN = 4
WALK = 2


def tile_smoothquant_error_moment_s12_kernel(
    tc, x, inv_c, w, ref, a_words, a_scales, b_words, b_scales, out
):
    nc = tc.nc
    with ExitStack() as ctx:
        keep = ctx.enter_context(tc.tile_pool(name="keep", bufs=1))
        stage = ctx.enter_context(tc.tile_pool(name="stage", bufs=3))
        work = ctx.enter_context(tc.psum_pool(name="work", bufs=4))
        moment = ctx.enter_context(tc.psum_pool(name="moment", bufs=1))
        ctx.enter_context(tc.manual_schedule())

        def kept(name, shape, dtype):
            return keep.tile(shape, dtype, name=name, align_bytes=64)

        b_codes = kept("b_codes", [P, KP, 2 * R], U8)
        b_plane = kept("b_plane", [P, KP, R], U8)
        a_rows_first = kept("a_rows_first", [P, KP, 2 * P], I32)
        a_rows_rest = kept("a_rows_rest", [P, KP, 2 * P], I32)
        a_raw = [kept("a_raw%d" % g, [P, KP, PASS // 2], I32) for g in range(GROUPS)]
        a_codes = [kept("a_codes%d" % g, [P, KP, PACK, 2 * P], U8) for g in range(GROUPS)]
        a_plane = [kept("a_plane%d" % g, [P, KP, PACK, P], U8) for g in range(GROUPS)]
        x_raw = [kept("x_raw%d" % g, [P, PACK, K], BF16) for g in range(GROUPS)]
        ref_raw = {
            (g, h): kept("ref_raw%d_%d" % (g, h), [P, PACK, HALF], BF16)
            for g in range(GROUPS)
            for h in range(N // HALF)
        }
        w_raw = [kept("w_raw%d" % h, [P, KP, PACK, HALF], BF16) for h in range(N // HALF)]
        inv = kept("inv", [P, KP, 2, 2], BF16)
        ident = kept("ident", [P, P], F32)
        xs_codes = [kept("xs_codes%d" % g, [P, KP, PASS], U32) for g in range(GROUPS)]
        xs_plane = [kept("xs_plane%d" % g, [P, KP, PASS], U8) for g in range(GROUPS)]
        w_codes = [kept("w_codes%d" % c, [P, KP, CH], U32) for c in range(N // CH)]
        w_plane = [kept("w_plane%d" % c, [P, KP, CH], U8) for c in range(N // CH)]
        f_codes = [kept("f_codes%d" % g, [P, R], U32) for g in range(GROUPS)]
        f_plane = [kept("f_plane%d" % g, [P, R], U8) for g in range(GROUPS)]

        nc.vector.memset(a_rows_first[:], 0)
        nc.vector.memset(a_rows_rest[:], 0)
        nc.gpsimd.memset(b_plane[:].rearrange("p g n -> p (g n)").bitcast(I32), 0)
        make_identity(nc, ident[:])

        a_words_g = a_words.bitcast(I32).rearrange("g p (G v) -> G p g v", G=GROUPS)
        a_scale_rows = a_scales.bitcast(I32).rearrange("g (q r) v -> r q g v", r=4)
        b_scale_rows = b_scales.bitcast(I32).rearrange("g (q r) v -> r q g v", r=4)
        x_rows = x.rearrange("(G s t r) k -> G r s t k", G=GROUPS, t=PACK, r=RUN)
        ref_rows = ref.rearrange("(G s t r) n -> G r s t n", G=GROUPS, t=PACK, r=RUN)
        w_rows = w.rearrange("(g p j) n -> g p j n", g=KP, j=PACK)

        def load_a(g):
            nc.sync.dma_start(out=a_raw[g][:], in_=a_words_g[g])

        def load_tokens(tiles, rows, g):
            for r in range(RUN):
                nc.sync.dma_start(out=tiles[g][r:P:RUN, :, :], in_=rows[g, r])

        def load_ref(g, h):
            for r in range(RUN):
                nc.sync.dma_start(
                    out=ref_raw[g, h][r:P:RUN, :, :], in_=ref_rows[g, r][:, :, h * HALF : (h + 1) * HALF]
                )

        def load_w(h, g):
            nc.sync.dma_start(out=w_raw[h][:, g], in_=w_rows[g][:, :, h * HALF : (h + 1) * HALF])

        def load_b():
            nc.sync.dma_start(
                out=b_codes[:].bitcast(I32), in_=b_words.bitcast(I32).rearrange("g p v -> p g v")
            )

        def load_a_scales(rows, first, count):
            for r in range(4):
                nc.sync.dma_start(
                    out=rows[r:P:32, :, :], in_=a_scale_rows[r][:, :, first * P : (first + count) * P]
                )

        def load_b_scales():
            for r in range(4):
                nc.sync.dma_start(out=b_plane[r:P:32, :, :].bitcast(I32), in_=b_scale_rows[r])

        def load_inv():
            nc.sync.dma_start(
                out=inv[:].rearrange("p g u e -> p g (u e)"),
                in_=inv_c.rearrange("(g p t) -> p g t", g=KP, t=PACK),
            )

        load_tokens(x_raw, x_rows, 0)
        load_a_scales(a_rows_first, 0, 2)
        load_inv()
        load_a(0)
        load_b()
        load_w(0, 0)
        load_b_scales()
        load_w(0, 1)
        load_a(1)
        load_ref(0, 0)
        load_tokens(x_raw, x_rows, 1)
        load_tokens(x_raw, x_rows, 2)
        load_a(2)
        load_a_scales(a_rows_rest, 2, 2)
        load_ref(1, 0)
        load_tokens(x_raw, x_rows, 3)
        load_a(3)
        load_ref(2, 0)
        load_w(1, 0)
        load_w(1, 1)
        load_ref(3, 0)
        for g in range(GROUPS):
            load_ref(g, 1)

        def order_a(g):
            rows = (a_rows_first, a_rows_rest)[g // 2][:, :, g % 2 * P : (g % 2 + 1) * P]
            nc.vector.tensor_copy(
                out=a_codes[g][:].bitcast(I32).rearrange("p g t (s h) -> p g t s h", h=2),
                in_=a_raw[g][:].rearrange("p g (s t h) -> p g t s h", t=PACK, h=2),
            )
            nc.vector.tensor_copy(
                out=a_plane[g][:].bitcast(I32).rearrange("p g t (b i) -> p g b t i", i=4),
                in_=rows.rearrange("p g (b i t) -> p g b t i", i=4, t=PACK),
            )

        def quantize(codes, plane, values):
            nc.vector.quantize_mx(out=codes.bitcast(FP8X4), scales=plane, in_=values)

        f_values = {}

        def features(g, c):
            if c == 0:
                f_values[g] = stage.tile([P, R, PACK], BF16, name="f_values", bufs=2, align_bytes=64)
            bank = work.tile([P, PACK * CH], F32, name="bank")
            for t in range(PACK):
                for kp in range(KP):
                    nc.tensor.matmul_mx(
                        out=bank[:, t * CH : (t + 1) * CH],
                        lhsT=a_codes[g][:, kp, t, :].bitcast(FP4X4),
                        lhsT_scale=a_plane[g][:, kp, t, :],
                        rhs=b_codes[:, kp, 2 * c * CH : 2 * (c + 1) * CH].bitcast(FP4X4),
                        rhs_scale=b_plane[:, kp, c * CH : (c + 1) * CH],
                        start=(kp == 0),
                        stop=(kp == KP - 1),
                    )
            nc.scalar.activation(
                out=f_values[g][:, c * CH : (c + 1) * CH, :],
                in_=bank[:].rearrange("p (t n) -> p n t", t=PACK),
                func=RELU,
            )

        def quantize_f(g):
            quantize(f_codes[g][:], f_plane[g][:], f_values[g][:].rearrange("p n t -> p (n t)"))

        x_sorted = {}

        def sort_x(g, kp):
            x_sorted[g, kp] = stage.tile([P, PACK, 2, P], F32, name="x_sorted")
            words = x_raw[g][:].bitcast(F32)[:, :, kp * 2 * P : (kp + 1) * 2 * P]
            nc.scalar.copy(out=x_sorted[g, kp][:], in_=words.rearrange("p t (v u) -> p t u v", u=2))

        xs_values = {}

        def turn_x(g, kp, pair):
            if pair == 0:
                xs_values[g, kp] = stage.tile([P, PASS, 2, 2], BF16, name="xs_values", align_bytes=64)
            bank = work.tile([P, PACK * CH], F32, name="bank")
            for u in range(2):
                for tt in range(2):
                    t = 2 * pair + tt
                    if (g, kp) in x_sorted:
                        words = x_sorted[g, kp][:, t, u, :]
                    else:
                        words = x_raw[g][:].bitcast(F32)[:, t, kp * 2 * P + u : (kp + 1) * 2 * P : 2]
                    at = (2 * u + tt) * P
                    nc.tensor.transpose(bank[:, at : at + P], words, ident[:])
            nc.vector.tensor_tensor(
                out=xs_values[g, kp][:, pair * 2 * P : (pair + 1) * 2 * P],
                in0=bank[:].bitcast(BF16).rearrange("p (u m e) -> p m u e", u=2, e=2),
                in1=inv[:, kp].unsqueeze(1).broadcast_to([P, 2 * P, 2, 2]),
                op=MULT,
            )

        def quantize_xs(g, kp):
            quantize(
                xs_codes[g][:, kp, :],
                xs_plane[g][:, kp, :],
                xs_values[g, kp][:].rearrange("p m u e -> p (m u e)"),
            )

        w_values = {}

        def interleave_w(c, on_vector):
            w_values[c] = stage.tile([P, KP, CH, PACK], BF16, name="w_values", bufs=4, align_bytes=64)
            h, n0 = divmod(c * CH, HALF)
            dst = w_values[c][:].rearrange("p g (b i) j -> p g b j i", i=4)
            src = w_raw[h][:, :, :, n0 : n0 + CH].rearrange("p g j (b i) -> p g b j i", i=4)
            if c == 0:
                for kp in range(KP):
                    nc.scalar.activation(out=dst[:, kp], in_=src[:, kp], func=COPY)
            elif on_vector:
                nc.vector.tensor_copy(out=dst, in_=src)
            else:
                nc.scalar.copy(out=dst, in_=src)

        def quantize_w(c):
            quantize(
                w_codes[c][:].rearrange("p g n -> p (g n)"),
                w_plane[c][:].rearrange("p g n -> p (g n)"),
                w_values[c][:].rearrange("p g n j -> p (g n j)"),
            )

        e_values, e_codes, e_plane = {}, {}, {}

        def error(g, c, span):
            n0, width = span
            at = c * CH - n0
            if at == 0:
                e_values[g, n0] = stage.tile([P, width, PACK], BF16, name="e_values", bufs=3, align_bytes=64)
            bank = work.tile([P, PACK * CH], F32, name="bank")
            for t in range(PACK):
                for kp in range(KP):
                    nc.tensor.matmul_mx(
                        out=bank[:, t * CH : (t + 1) * CH],
                        lhsT=xs_codes[g][:, kp, t * P : (t + 1) * P].bitcast(FP8X4),
                        lhsT_scale=xs_plane[g][:, kp, t * P : (t + 1) * P],
                        rhs=w_codes[c][:, kp, :].bitcast(FP8X4),
                        rhs_scale=w_plane[c][:, kp, :],
                        start=(kp == 0),
                        stop=(kp == KP - 1),
                    )
            nc.vector.tensor_tensor(
                out=e_values[g, n0][:, at : at + CH, :].rearrange("p (b i) t -> p b t i", i=WALK),
                in0=bank[:].rearrange("p (t b i) -> p b t i", t=PACK, i=WALK),
                in1=ref_raw[g, c * CH // HALF][:, :, c * CH % HALF : c * CH % HALF + CH].rearrange("p t (b i) -> p b t i", i=WALK),
                op=SUB,
            )

        def quantize_e(g, span):
            n0, width = span
            e_codes[g, n0] = stage.tile([P, width], U32, name="e_codes", bufs=5, align_bytes=64)
            e_plane[g, n0] = stage.tile([P, width], U8, name="e_plane", bufs=5, align_bytes=64)
            quantize(e_codes[g, n0][:], e_plane[g, n0][:], e_values[g, n0][:].rearrange("p n t -> p (n t)"))

        sums = {}

        def moment_pass(g, span, rt):
            n0, width = span
            if g == 0:
                sums[n0, rt] = moment.tile([P, HALF], F32, name="sums%d" % rt)
            nc.tensor.matmul_mx(
                out=sums[n0, rt][:, 0:width],
                lhsT=f_codes[g][:, rt * P : (rt + 1) * P].bitcast(FP8X4),
                lhsT_scale=f_plane[g][:, rt * P : (rt + 1) * P],
                rhs=e_codes[g, n0][:].bitcast(FP8X4),
                rhs_scale=e_plane[g, n0][:],
                start=(g == 0),
                stop=(g == GROUPS - 1),
            )

        def moment_passes(g, span):
            for rt in range(R // P):
                moment_pass(g, span, rt)

        def store(span, rt, on_vector):
            n0, width = span
            result = stage.tile([P, width], F32, name="result", bufs=4)
            if on_vector:
                nc.vector.tensor_copy(out=result[:], in_=sums[n0, rt][:, 0:width])
            else:
                nc.scalar.copy(out=result[:], in_=sums[n0, rt][:, 0:width])
            nc.sync.dma_start(out=out[rt * P : (rt + 1) * P, n0 : n0 + width], in_=result[:])

        def errors(g, span, between):
            n0, width = span
            for i in range(width // CH):
                error(g, n0 // CH + i, span)
                for step in between.get(i, ()):
                    step()

        def turn_group(g, between):
            for i in range(4):
                turn_x(g, i // 2, i % 2)
                for step in between.get(i, ()):
                    step()

        def do(fn, *args):
            return lambda: fn(*args)

        first, third, last = (0, 512), (512, 256), (768, 256)
        sort_x(0, 1)
        turn_group(0, {0: [do(order_a, 0)]})
        interleave_w(0, False)
        interleave_w(1, False)
        for c in range(4):
            features(0, c)
        quantize_xs(0, 0)
        interleave_w(2, True)
        quantize_xs(0, 1)
        quantize_w(0)
        interleave_w(3, True)
        quantize_w(1)
        quantize_w(2)
        quantize_w(3)
        order_a(1)
        sort_x(1, 1)

        for g in range(GROUPS - 1):
            errors(g, first, {})
            turn_group(g + 1, {})
            if g > 0:
                moment_passes(g - 1, first)
            if g + 2 == GROUPS:
                interleave_w(4, False)
                interleave_w(5, False)
            for c in range(4):
                features(g + 1, c)
            quantize_xs(g + 1, 0)
            quantize_xs(g + 1, 1)
            quantize_e(g, first)
            quantize_f(g)
            if g + 2 < GROUPS:
                sort_x(g + 2, 0)
                sort_x(g + 2, 1)
                order_a(g + 2)
            else:
                quantize_w(4)
                quantize_w(5)

        interleave_w(6, False)
        interleave_w(7, False)
        errors(3, first, {})
        moment_passes(2, first)
        quantize_f(3)
        quantize_e(3, first)
        errors(0, third, {})
        errors(1, third, {0: [do(quantize_e, 0, third)]})
        moment_passes(3, first)
        for rt in range(4):
            store(first, rt, False)
        errors(2, third, {0: [do(quantize_e, 1, third), do(quantize_w, 6)]})
        errors(3, third, {0: [do(quantize_e, 2, third), do(quantize_w, 7)]})
        moment_passes(0, third)
        moment_passes(1, third)
        errors(0, last, {0: [do(quantize_e, 3, third)]})
        moment_passes(2, third)
        errors(1, last, {0: [do(quantize_e, 0, last)]})
        moment_passes(3, third)
        for rt in range(4):
            store(third, rt, False)
        errors(2, last, {0: [do(quantize_e, 1, last)]})
        errors(3, last, {0: [do(quantize_e, 2, last)]})
        quantize_e(3, last)
        for g in range(3):
            moment_passes(g, last)
        for rt in range(4):
            moment_pass(3, last, rt)
            store(last, rt, rt % 2 == 1)
